import numpy as np
import ml_dtypes


def mxq(x, axis, fmt="e4m3"):
    dtype, down = {"e4m3": (ml_dtypes.float8_e4m3fn, 7), "e5m2": (ml_dtypes.float8_e5m2, 14)}[fmt]
    v = np.moveaxis(np.asarray(x, np.float32).astype(ml_dtypes.bfloat16).astype(np.float64), axis, -1)
    blocks = v.reshape(v.shape[:-1] + (-1, 32))
    amax = np.abs(blocks).max(-1, keepdims=True)
    byte = np.maximum(np.where(amax > 0, np.frexp(amax)[1] - 1 + 127, 0) - down, 1)
    scale = np.exp2(byte - 127.0)
    codes = (blocks / scale).astype(np.float32).astype(dtype).astype(np.float64)
    return np.moveaxis((codes * scale).reshape(v.shape), -1, axis)


WIDE = False


def mx_kscale(k, group=512):
    if not WIDE:
        return np.ones(k)
    levels = np.array([18, -18])
    if group != 512:
        return np.exp2(np.random.permutation(np.resize(levels, k // group))).repeat(group)
    if k % 512:
        return np.exp2(np.random.permutation(np.resize(levels, k // 32))).repeat(32)
    a = np.empty((k // 512, 16))
    for p in range(k // 512):
        a[p, :8] = np.random.permutation(np.resize(levels, 8))
        for g in range(8):
            far = levels[np.abs(levels - a[p, g]) >= 10]
            a[p, g + 8] = far[np.random.randint(len(far))]
    return np.exp2(a.ravel()).repeat(32)


def f64(x):
    return np.asarray(x).astype(np.float64)


K, R, M, N = 1024, 128, 512, 512


def setup_inputs():
    n = np.random.standard_normal
    s = mx_kscale(K)[:, None]
    z = mx_kscale(R, 0)
    return {
        "x": (n((K, N)) * s).astype(np.float32),
        "w": (n((K, M)) / np.sqrt(K) / s).astype(np.float32),
        "a": (n((K, R)) / np.sqrt(K) / s * z).astype(np.float32),
        "bb": (n((R, M)) / np.sqrt(R) / z[:, None]).astype(np.float32),
    }


def reference(x, w, a, bb):
    xq = mxq(f64(x), 0, "e4m3")
    z = mxq(f64(a), 0, "e4m3").T @ xq
    y = (mxq(f64(w), 0, "e4m3").T @ xq) + (mxq(f64(bb), 0, "e4m3").T @ mxq(z, 0, "e4m3"))
    y = np.tanh(y)
    return y

@@ -1,0 +1,215 @@
+from contextlib import ExitStack
+
+import concourse.mybir as mybir
+
+K, R, M, N = 1024, 128, 512, 512
+FLOPS = 2 * K * M * N + 2 * K * R * N + 2 * R * M * N
+
+F32 = mybir.dt.float32
+BF16 = mybir.dt.bfloat16
+I32 = mybir.dt.int32
+U8 = mybir.dt.uint8
+FP8X4 = mybir.dt.float8_e4m3fn_x4
+TANH = mybir.ActivationFunctionType.Tanh
+ADD = mybir.AluOpType.add
+
+P = 128
+PACK = 4
+K_PASS = P * PACK
+PASSES = K // K_PASS
+ROWS = R // PACK
+C = 128
+TILES = 4
+BB_SPLIT = 320
+
+
+def tile_rows_lora_tanh_kernel(tc, x, w, a, bb, out):
+    nc = tc.nc
+    with ExitStack() as ctx:
+        sb = ctx.enter_context(tc.tile_pool(name="sb", bufs=1))
+        ps = ctx.enter_context(tc.psum_pool(name="ps", bufs=1))
+        ctx.enter_context(tc.manual_schedule())
+
+        def sbuf(name, shape, dtype):
+            return sb.tile(shape, dtype, name=name, align_bytes=64)
+
+        def copy(engine, dst, src):
+            if engine == "v":
+                nc.vector.tensor_copy(out=dst, in_=src)
+            else:
+                nc.scalar.copy(out=dst, in_=src)
+
+        def interleave(engine, dst, src):
+            copy(engine, dst.rearrange("p (c i) j -> p c j i", i=4), src.rearrange("p j (c i) -> p c j i", i=4))
+
+        def quantize(codes, scales, src):
+            nc.vector.quantize_mx(out=codes.bitcast(FP8X4), scales=scales, in_=src.rearrange("p c j -> p (c j)"))
+
+        def mx(dst, lhs, rhs, start, stop):
+            nc.tensor.matmul_mx(out=dst, lhsT=lhs[0].bitcast(FP8X4), lhsT_scale=lhs[1],
+                                rhs=rhs[0].bitcast(FP8X4), rhs_scale=rhs[1], start=start, stop=stop)
+
+        class_tiles = {}
+
+        def operand(name):
+            bf = sbuf(name + "_bf", [P, C, PACK], BF16)
+            codes = sbuf(name + "_codes", [P, C], I32)
+            scales = sbuf(name + "_scales", [P, C], U8)
+            class_tiles[name] = (bf, codes, scales)
+
+        for g in range(PASSES):
+            operand("a%d" % g)
+            for t in range(TILES):
+                operand("x%d%d" % (g, t))
+                operand("w%d%d" % (g, t))
+        operand("z")
+
+        def q(name):
+            bf, codes, scales = class_tiles[name]
+            quantize(codes[:], scales[:], bf[:])
+
+        def op(name):
+            return (class_tiles[name][1][:], class_tiles[name][2][:])
+
+        full = [ps.tile([P, 512], F32, name="full%d" % i) for i in range(4)]
+        rowb = [ps.tile([P, 512], F32, name="row%d" % i) for i in range(4)]
+
+        bb_raw = sbuf("bb_raw", [ROWS, PACK, M], F32)
+        bb_bf = sbuf("bb_bf", [ROWS, M, PACK], BF16)
+        bb_mx = [sbuf("bb_mx%d" % i, [P, M + M // 4], I32) for i in range(4)]
+        x_raw = [sbuf("x_raw%d" % g, [P, PACK, N], F32) for g in range(PASSES)]
+        a_raw = sbuf("a_raw", [P, PASSES, PACK, R], F32)
+        w_raw = {}
+
+        def load_w(g, t0, t1):
+            raw = sbuf("w_raw%d%d" % (g, t0), [P, PACK, (t1 - t0) * C], F32)
+            nc.sync.dma_start(out=raw[:], in_=w[g * K_PASS:(g + 1) * K_PASS, t0 * C:t1 * C].rearrange("(p j) m -> p j m", j=PACK))
+            for t in range(t0, t1):
+                w_raw[g, t] = raw[:, :, (t - t0) * C:(t - t0 + 1) * C]
+
+        def load_x(g):
+            nc.sync.dma_start(out=x_raw[g][:], in_=x[g * K_PASS:(g + 1) * K_PASS, :].rearrange("(p j) n -> p j n", j=PACK))
+
+        def cx(e, g, t):
+            interleave(e, class_tiles["x%d%d" % (g, t)][0][:], x_raw[g][:, :, t * C:(t + 1) * C])
+
+        def cw(e, g, t):
+            interleave(e, class_tiles["w%d%d" % (g, t)][0][:], w_raw[g, t])
+
+        def ca(e, g):
+            copy(e, class_tiles["a%d" % g][0][:].rearrange("p (b i) j -> p i j b", b=PACK),
+                 a_raw[:, g, :, :].rearrange("p j (i b) -> p i j b", b=PACK))
+
+        def zmm(g, t):
+            mx(full[t][:, 0:R], op("x%d%d" % (g, t)), op("a%d" % g), g == 0, g == PASSES - 1)
+
+        nc.vector.memset(bb_mx[0][:, M:], 0)
+        nc.sync.dma_start(out=bb_raw[:], in_=bb.rearrange("(p j) m -> p j m", j=PACK))
+        load_x(0)
+        nc.sync.dma_start(out=a_raw[:], in_=a.rearrange("(g p j) r -> p g j r", g=PASSES, j=PACK))
+        load_x(1)
+        load_w(0, 0, 2)
+
+        interleave("v", bb_bf[:, 0:BB_SPLIT, :], bb_raw[:, :, 0:BB_SPLIT])
+        interleave("s", bb_bf[:, BB_SPLIT:, :], bb_raw[:, :, BB_SPLIT:])
+        quantize(bb_mx[0][0:ROWS, 0:M], bb_mx[0][0:ROWS, M:].bitcast(U8), bb_bf[:])
+        for i in range(1, 4):
+            nc.sync.dma_start(out=bb_mx[i][ROWS * i:ROWS * (i + 1), :], in_=bb_mx[0][0:ROWS, :])
+        load_w(1, 0, 2)
+        load_w(0, 2, 4)
+        load_w(1, 2, 3)
+        load_w(1, 3, 4)
+
+        cx("v", 0, 0)
+        cx("s", 0, 2)
+        cx("v", 0, 1)
+        cx("s", 0, 3)
+        for t in range(4):
+            q("x0%d" % t)
+        ca("v", 0)
+        ca("s", 1)
+        q("a0")
+        q("a1")
+        for t in range(4):
+            zmm(0, t)
+
+        cx("v", 1, 0)
+        cx("s", 1, 1)
+        cx("v", 1, 2)
+        cx("s", 1, 3)
+        for t in range(4):
+            q("x1%d" % t)
+            zmm(1, t)
+        cw("s", 0, 0)
+        cw("s", 0, 1)
+        z_t = sbuf("z_t", [P, TILES, R], F32)
+        for t in range(4):
+            nc.vector.transpose(out=z_t[:, t, :], in_=full[t][:, 0:R])
+        q("w00")
+        nc.vector.tensor_copy(out=class_tiles["z"][0][:].rearrange("p (t c i) b -> p t c b i", t=TILES, i=4),
+                              in_=z_t[:].rearrange("p t (b c i) -> p t c b i", b=PACK, i=4))
+        q("w01")
+        q("z")
+        z_codes, z_scales = class_tiles["z"][1], class_tiles["z"][2]
+        for mt in range(4):
+            for i in range(4):
+                rows = slice(ROWS * i, ROWS * (i + 1))
+                lhs = (bb_mx[i][rows, mt * C:(mt + 1) * C], bb_mx[i][rows, M:].bitcast(U8)[:, mt * C:(mt + 1) * C])
+                mx(rowb[i][:, mt * C:(mt + 1) * C], lhs, (z_codes[rows, :], z_scales[rows, :]), True, True)
+
+        cw("s", 1, 0)
+        cw("v", 1, 1)
+        q("w10")
+        q("w11")
+
+        low = [sbuf("low%d" % h, [P, 4, 2 * C], F32) for h in range(2)]
+
+        def lcopy(h):
+            for i in range(4):
+                nc.scalar.copy(out=low[h][:, i, :], in_=rowb[i][:, 2 * C * h:2 * C * (h + 1)])
+
+        def wmm(mt, t0, t1, bank):
+            for t in range(t0, t1):
+                for g in range(PASSES):
+                    mx(full[bank][:, (t - t0) * C:(t - t0 + 1) * C], op("w%d%d" % (g, mt)), op("x%d%d" % (g, t)), g == 0, g == PASSES - 1)
+
+        ysum = {}
+
+        def add(mt, t0, t1, bank):
+            y = sbuf("y%d%d" % (mt, t0), [P, (t1 - t0) * C], F32)
+            ysum[mt, t0] = y
+            lo = low[mt // 2][:, :, (mt % 2) * C:(mt % 2 + 1) * C].rearrange("p i (t j) -> p t i j", j=ROWS)[:, t0:t1]
+            nc.vector.tensor_tensor(out=y[:].rearrange("p (t i j) -> p t i j", i=4, j=ROWS),
+                                    in0=full[bank][:, 0:(t1 - t0) * C].rearrange("p (t i j) -> p t i j", i=4, j=ROWS),
+                                    in1=lo, op=ADD)
+
+        def finish(mt, t0, t1):
+            res = sbuf("res%d%d" % (mt, t0), [P, (t1 - t0) * C], F32)
+            nc.scalar.activation(out=res[:], in_=ysum[mt, t0][:], func=TANH)
+            nc.sync.dma_start(out=out[mt * C:(mt + 1) * C, t0 * C:t1 * C], in_=res[:])
+
+        wmm(0, 0, 4, 0)
+        wmm(1, 0, 4, 1)
+        lcopy(0)
+        cw("v", 0, 2)
+        cw("v", 0, 3)
+        q("w02")
+        q("w03")
+        lcopy(1)
+        cw("v", 1, 2)
+        add(0, 0, 4, 0)
+        q("w12")
+        wmm(2, 0, 4, 2)
+        cw("v", 1, 3)
+        finish(0, 0, 4)
+        add(1, 0, 4, 1)
+        q("w13")
+        wmm(3, 0, 2, 3)
+        wmm(3, 2, 4, 0)
+        finish(1, 0, 4)
+        add(2, 0, 4, 2)
+        finish(2, 0, 4)
+        add(3, 0, 2, 3)
+        finish(3, 0, 2)
+        add(3, 2, 4, 0)
+        finish(3, 2, 4)

@@ -108,7 +108,7 @@ def tile_rows_lora_tanh_kernel(tc, x, w, a, bb, out):
         load_x(0)
         nc.sync.dma_start(out=a_raw[:], in_=a.rearrange("(g p j) r -> p g j r", g=PASSES, j=PACK))
         load_x(1)
-        load_w(0, 0, 2)
+        load_w(0, 0, 4)
 
         interleave("v", bb_bf[:, 0:BB_SPLIT, :], bb_raw[:, :, 0:BB_SPLIT])
         interleave("s", bb_bf[:, BB_SPLIT:, :], bb_raw[:, :, BB_SPLIT:])
@@ -116,9 +116,7 @@ def tile_rows_lora_tanh_kernel(tc, x, w, a, bb, out):
         for i in range(1, 4):
             nc.sync.dma_start(out=bb_mx[i][ROWS * i:ROWS * (i + 1), :], in_=bb_mx[0][0:ROWS, :])
         load_w(1, 0, 2)
-        load_w(0, 2, 4)
-        load_w(1, 2, 3)
-        load_w(1, 3, 4)
+        load_w(1, 2, 4)
 
         cx("v", 0, 0)
         cx("s", 0, 2)
@@ -140,15 +138,26 @@ def tile_rows_lora_tanh_kernel(tc, x, w, a, bb, out):
         for t in range(4):
             q("x1%d" % t)
             zmm(1, t)
+        z_t = sbuf("z_t", [P, TILES, R], F32)
+
+        def turn(t):
+            nc.vector.transpose(out=z_t[:, t, :], in_=full[t][:, 0:R])
+
+        def cz(t0, t1):
+            nc.vector.tensor_copy(out=class_tiles["z"][0][:].rearrange("p (t c i) b -> p t c b i", t=TILES, i=4)[:, t0:t1],
+                                  in_=z_t[:].rearrange("p t (b c i) -> p t c b i", b=PACK, i=4)[:, t0:t1])
+
+        turn(0)
+        turn(1)
+        turn(2)
+        cz(0, 2)
+        turn(3)
         cw("s", 0, 0)
         cw("s", 0, 1)
-        z_t = sbuf("z_t", [P, TILES, R], F32)
-        for t in range(4):
-            nc.vector.transpose(out=z_t[:, t, :], in_=full[t][:, 0:R])
+        cw("s", 0, 3)
+        cw("v", 0, 2)
+        cz(2, 4)
         q("w00")
-        nc.vector.tensor_copy(out=class_tiles["z"][0][:].rearrange("p (t c i) b -> p t c b i", t=TILES, i=4),
-                              in_=z_t[:].rearrange("p t (b c i) -> p t c b i", b=PACK, i=4))
-        q("w01")
         q("z")
         z_codes, z_scales = class_tiles["z"][1], class_tiles["z"][2]
         for mt in range(4):
@@ -157,16 +166,10 @@ def tile_rows_lora_tanh_kernel(tc, x, w, a, bb, out):
                 lhs = (bb_mx[i][rows, mt * C:(mt + 1) * C], bb_mx[i][rows, M:].bitcast(U8)[:, mt * C:(mt + 1) * C])
                 mx(rowb[i][:, mt * C:(mt + 1) * C], lhs, (z_codes[rows, :], z_scales[rows, :]), True, True)
 
-        cw("s", 1, 0)
-        cw("v", 1, 1)
-        q("w10")
-        q("w11")
-
         low = [sbuf("low%d" % h, [P, 4, 2 * C], F32) for h in range(2)]
 
-        def lcopy(h):
-            for i in range(4):
-                nc.scalar.copy(out=low[h][:, i, :], in_=rowb[i][:, 2 * C * h:2 * C * (h + 1)])
+        def lcopy(e, i, h):
+            copy(e, low[h][:, i, :], rowb[i][:, 2 * C * h:2 * C * (h + 1)])
 
         def wmm(mt, t0, t1, bank):
             for t in range(t0, t1):
@@ -183,33 +186,56 @@ def tile_rows_lora_tanh_kernel(tc, x, w, a, bb, out):
                                     in0=full[bank][:, 0:(t1 - t0) * C].rearrange("p (t i j) -> p t i j", i=4, j=ROWS),
                                     in1=lo, op=ADD)
 
-        def finish(mt, t0, t1):
-            res = sbuf("res%d%d" % (mt, t0), [P, (t1 - t0) * C], F32)
-            nc.scalar.activation(out=res[:], in_=ysum[mt, t0][:], func=TANH)
-            nc.sync.dma_start(out=out[mt * C:(mt + 1) * C, t0 * C:t1 * C], in_=res[:])
+        def m(mt, h):
+            wmm(mt, 2 * h, 2 * h + 2, (2 * mt + h) % 4)
 
-        wmm(0, 0, 4, 0)
-        wmm(1, 0, 4, 1)
-        lcopy(0)
-        cw("v", 0, 2)
-        cw("v", 0, 3)
+        def ad(mt, h):
+            add(mt, 2 * h, 2 * h + 2, (2 * mt + h) % 4)
+
+        res = [sbuf("res%d" % mt, [P, N], F32) for mt in range(4)]
+
+        def th(mt, h):
+            cols = slice(2 * C * h, 2 * C * (h + 1))
+            nc.scalar.activation(out=res[mt][:, cols], in_=ysum[mt, 2 * h][:], func=TANH)
+            if mt == 3:
+                nc.sync.dma_start(out=out[mt * C:(mt + 1) * C, cols], in_=res[mt][:, cols])
+            elif h == 1:
+                nc.sync.dma_start(out=out[mt * C:(mt + 1) * C, :], in_=res[mt][:])
+
         q("w02")
+        q("w01")
+        cw("v", 1, 0)
         q("w03")
-        lcopy(1)
+        q("w10")
+        cw("v", 1, 1)
+        for i in range(3):
+            lcopy("s", i, 0)
+        m(0, 0)
+        m(0, 1)
+        lcopy("v", 3, 0)
+        q("w11")
+        m(1, 0)
+        m(1, 1)
+        for i in range(4):
+            lcopy("s", i, 1)
         cw("v", 1, 2)
-        add(0, 0, 4, 0)
+        ad(0, 0)
         q("w12")
-        wmm(2, 0, 4, 2)
         cw("v", 1, 3)
-        finish(0, 0, 4)
-        add(1, 0, 4, 1)
+        ad(0, 1)
         q("w13")
-        wmm(3, 0, 2, 3)
-        wmm(3, 2, 4, 0)
-        finish(1, 0, 4)
-        add(2, 0, 4, 2)
-        finish(2, 0, 4)
-        add(3, 0, 2, 3)
-        finish(3, 0, 2)
-        add(3, 2, 4, 0)
-        finish(3, 2, 4)
+        m(2, 0)
+        m(2, 1)
+        ad(1, 0)
+        ad(1, 1)
+        m(3, 0)
+        m(3, 1)
+        th(0, 0)
+        th(0, 1)
+        th(1, 0)
+        th(1, 1)
+        for mt in range(2, 4):
+            ad(mt, 0)
+            ad(mt, 1)
+            th(mt, 0)
+            th(mt, 1)

@@ -154,27 +154,28 @@ def tile_rows_lora_tanh_kernel(tc, x, w, a, bb, out):
         turn(3)
         cw("s", 0, 0)
         cw("s", 0, 1)
-        cw("s", 0, 3)
         cw("v", 0, 2)
         cz(2, 4)
         q("w00")
         q("z")
         z_codes, z_scales = class_tiles["z"][1], class_tiles["z"][2]
-        for mt in range(4):
-            for i in range(4):
-                rows = slice(ROWS * i, ROWS * (i + 1))
-                lhs = (bb_mx[i][rows, mt * C:(mt + 1) * C], bb_mx[i][rows, M:].bitcast(U8)[:, mt * C:(mt + 1) * C])
-                mx(rowb[i][:, mt * C:(mt + 1) * C], lhs, (z_codes[rows, :], z_scales[rows, :]), True, True)
+
+        def rmm():
+            for mt in range(4):
+                for i in range(4):
+                    rows = slice(ROWS * i, ROWS * (i + 1))
+                    lhs = (bb_mx[i][rows, mt * C:(mt + 1) * C], bb_mx[i][rows, M:].bitcast(U8)[:, mt * C:(mt + 1) * C])
+                    mx(rowb[i][:, mt * C:(mt + 1) * C], lhs, (z_codes[rows, :], z_scales[rows, :]), True, True)
 
         low = [sbuf("low%d" % h, [P, 4, 2 * C], F32) for h in range(2)]
 
         def lcopy(e, i, h):
             copy(e, low[h][:, i, :], rowb[i][:, 2 * C * h:2 * C * (h + 1)])
 
-        def wmm(mt, t0, t1, bank):
-            for t in range(t0, t1):
-                for g in range(PASSES):
-                    mx(full[bank][:, (t - t0) * C:(t - t0 + 1) * C], op("w%d%d" % (g, mt)), op("x%d%d" % (g, t)), g == 0, g == PASSES - 1)
+        def wmm(g, mt):
+            for t in range(TILES):
+                mx(full[mt][:, t * C:(t + 1) * C], op("w%d%d" % (g, mt)), op("x%d%d" % (g, t)),
+                   g == 0 and t == 0, g == PASSES - 1 and t == TILES - 1)
 
         ysum = {}
 
@@ -183,59 +184,61 @@ def tile_rows_lora_tanh_kernel(tc, x, w, a, bb, out):
             ysum[mt, t0] = y
             lo = low[mt // 2][:, :, (mt % 2) * C:(mt % 2 + 1) * C].rearrange("p i (t j) -> p t i j", j=ROWS)[:, t0:t1]
             nc.vector.tensor_tensor(out=y[:].rearrange("p (t i j) -> p t i j", i=4, j=ROWS),
-                                    in0=full[bank][:, 0:(t1 - t0) * C].rearrange("p (t i j) -> p t i j", i=4, j=ROWS),
+                                    in0=full[bank][:, t0 * C:t1 * C].rearrange("p (t i j) -> p t i j", i=4, j=ROWS),
                                     in1=lo, op=ADD)
 
-        def m(mt, h):
-            wmm(mt, 2 * h, 2 * h + 2, (2 * mt + h) % 4)
-
-        def ad(mt, h):
-            add(mt, 2 * h, 2 * h + 2, (2 * mt + h) % 4)
+        def ad(mt, t0, t1):
+            add(mt, t0, t1, mt)
 
         res = [sbuf("res%d" % mt, [P, N], F32) for mt in range(4)]
 
-        def th(mt, h):
-            cols = slice(2 * C * h, 2 * C * (h + 1))
-            nc.scalar.activation(out=res[mt][:, cols], in_=ysum[mt, 2 * h][:], func=TANH)
-            if mt == 3:
+        def th(mt, t0, t1):
+            nc.scalar.activation(out=res[mt][:, t0 * C:t1 * C], in_=ysum[mt, t0][:], func=TANH)
+            if t1 % 2 == 0:
+                cols = slice((t1 - 2) * C, t1 * C)
                 nc.sync.dma_start(out=out[mt * C:(mt + 1) * C, cols], in_=res[mt][:, cols])
-            elif h == 1:
-                nc.sync.dma_start(out=out[mt * C:(mt + 1) * C, :], in_=res[mt][:])
 
-        q("w02")
+        rmm()
+        wmm(0, 0)
+        cw("v", 0, 3)
         q("w01")
-        cw("v", 1, 0)
+        wmm(0, 1)
+        q("w02")
         q("w03")
-        q("w10")
-        cw("v", 1, 1)
-        for i in range(3):
-            lcopy("s", i, 0)
-        m(0, 0)
-        m(0, 1)
-        lcopy("v", 3, 0)
-        q("w11")
-        m(1, 0)
-        m(1, 1)
+        cw("v", 1, 0)
         for i in range(4):
+            lcopy("s", i, 0)
+        cw("v", 1, 1)
+        q("w10")
+        wmm(1, 0)
+        q("w11")
+        wmm(1, 1)
+        wmm(0, 2)
+        wmm(0, 3)
+        lcopy("v", 3, 1)
+        for i in range(3):
             lcopy("s", i, 1)
         cw("v", 1, 2)
-        ad(0, 0)
+        ad(0, 0, 2)
+        cw("s", 1, 3)
         q("w12")
-        cw("v", 1, 3)
-        ad(0, 1)
+        wmm(1, 2)
+        ad(0, 2, 4)
+        th(0, 0, 2)
+        th(0, 2, 4)
+        ad(1, 0, 2)
         q("w13")
-        m(2, 0)
-        m(2, 1)
-        ad(1, 0)
-        ad(1, 1)
-        m(3, 0)
-        m(3, 1)
-        th(0, 0)
-        th(0, 1)
-        th(1, 0)
-        th(1, 1)
-        for mt in range(2, 4):
-            ad(mt, 0)
-            ad(mt, 1)
-            th(mt, 0)
-            th(mt, 1)
+        wmm(1, 3)
+        ad(1, 2, 4)
+        th(1, 0, 2)
+        th(1, 2, 4)
+        ad(2, 0, 2)
+        ad(2, 2, 4)
+        th(2, 0, 2)
+        th(2, 2, 4)
+        ad(3, 0, 2)
+        ad(3, 2, 3)
+        ad(3, 3, 4)
+        th(3, 0, 2)
+        th(3, 2, 3)
+        th(3, 3, 4)

@@ -148,21 +148,23 @@ def tile_rows_lora_tanh_kernel(tc, x, w, a, bb, out):
                                   in_=z_t[:].rearrange("p t (b c i) -> p t c b i", b=PACK, i=4)[:, t0:t1])
 
         turn(0)
+        for i in range(11):
+            mx(full[0][:, C * (i % 4):C * (i % 4 + 1)], op("x00"), op("a0"), True, True)
         turn(1)
         turn(2)
-        cz(0, 2)
         turn(3)
         cw("s", 0, 0)
         cw("s", 0, 1)
-        cw("v", 0, 2)
+        cw("s", 0, 2)
+        cz(0, 2)
         cz(2, 4)
         q("w00")
         q("z")
         z_codes, z_scales = class_tiles["z"][1], class_tiles["z"][2]
 
         def rmm():
-            for mt in range(4):
-                for i in range(4):
+            for i in range(4):
+                for mt in range(4):
                     rows = slice(ROWS * i, ROWS * (i + 1))
                     lhs = (bb_mx[i][rows, mt * C:(mt + 1) * C], bb_mx[i][rows, M:].bitcast(U8)[:, mt * C:(mt + 1) * C])
                     mx(rowb[i][:, mt * C:(mt + 1) * C], lhs, (z_codes[rows, :], z_scales[rows, :]), True, True)
@@ -203,12 +205,12 @@ def tile_rows_lora_tanh_kernel(tc, x, w, a, bb, out):
         cw("v", 0, 3)
         q("w01")
         wmm(0, 1)
-        q("w02")
         q("w03")
+        q("w02")
         cw("v", 1, 0)
+        cw("v", 1, 1)
         for i in range(4):
             lcopy("s", i, 0)
-        cw("v", 1, 1)
         q("w10")
         wmm(1, 0)
         q("w11")
@@ -216,29 +218,21 @@ def tile_rows_lora_tanh_kernel(tc, x, w, a, bb, out):
         wmm(0, 2)
         wmm(0, 3)
         lcopy("v", 3, 1)
-        for i in range(3):
-            lcopy("s", i, 1)
+        lcopy("s", 0, 1)
+        lcopy("s", 1, 1)
         cw("v", 1, 2)
         ad(0, 0, 2)
         cw("s", 1, 3)
+        lcopy("s", 2, 1)
+        ad(0, 2, 4)
         q("w12")
         wmm(1, 2)
-        ad(0, 2, 4)
         th(0, 0, 2)
         th(0, 2, 4)
-        ad(1, 0, 2)
         q("w13")
         wmm(1, 3)
-        ad(1, 2, 4)
-        th(1, 0, 2)
-        th(1, 2, 4)
-        ad(2, 0, 2)
-        ad(2, 2, 4)
-        th(2, 0, 2)
-        th(2, 2, 4)
-        ad(3, 0, 2)
-        ad(3, 2, 3)
-        ad(3, 3, 4)
-        th(3, 0, 2)
-        th(3, 2, 3)
-        th(3, 3, 4)
+        for mt in range(1, 4):
+            ad(mt, 0, 2)
+            ad(mt, 2, 4)
+            th(mt, 0, 2)
+            th(mt, 2, 4)

from contextlib import ExitStack

import concourse.mybir as mybir

K, R, M, N = 1024, 128, 512, 512
FLOPS = 2 * K * M * N + 2 * K * R * N + 2 * R * M * N

F32 = mybir.dt.float32
BF16 = mybir.dt.bfloat16
I32 = mybir.dt.int32
U8 = mybir.dt.uint8
FP8X4 = mybir.dt.float8_e4m3fn_x4
TANH = mybir.ActivationFunctionType.Tanh
ADD = mybir.AluOpType.add

P = 128
PACK = 4
K_PASS = P * PACK
PASSES = K // K_PASS
ROWS = R // PACK
C = 128
TILES = 4
BB_SPLIT = 320


def tile_rows_lora_tanh_kernel(tc, x, w, a, bb, out):
    nc = tc.nc
    with ExitStack() as ctx:
        sb = ctx.enter_context(tc.tile_pool(name="sb", bufs=1))
        ps = ctx.enter_context(tc.psum_pool(name="ps", bufs=1))
        ctx.enter_context(tc.manual_schedule())

        def sbuf(name, shape, dtype):
            return sb.tile(shape, dtype, name=name, align_bytes=64)

        def copy(engine, dst, src):
            if engine == "v":
                nc.vector.tensor_copy(out=dst, in_=src)
            else:
                nc.scalar.copy(out=dst, in_=src)

        def interleave(engine, dst, src):
            copy(engine, dst.rearrange("p (c i) j -> p c j i", i=4), src.rearrange("p j (c i) -> p c j i", i=4))

        def quantize(codes, scales, src):
            nc.vector.quantize_mx(out=codes.bitcast(FP8X4), scales=scales, in_=src.rearrange("p c j -> p (c j)"))

        def mx(dst, lhs, rhs, start, stop):
            nc.tensor.matmul_mx(out=dst, lhsT=lhs[0].bitcast(FP8X4), lhsT_scale=lhs[1],
                                rhs=rhs[0].bitcast(FP8X4), rhs_scale=rhs[1], start=start, stop=stop)

        class_tiles = {}

        def operand(name):
            bf = sbuf(name + "_bf", [P, C, PACK], BF16)
            codes = sbuf(name + "_codes", [P, C], I32)
            scales = sbuf(name + "_scales", [P, C], U8)
            class_tiles[name] = (bf, codes, scales)

        for g in range(PASSES):
            operand("a%d" % g)
            for t in range(TILES):
                operand("x%d%d" % (g, t))
                operand("w%d%d" % (g, t))
        operand("z")

        def q(name):
            bf, codes, scales = class_tiles[name]
            quantize(codes[:], scales[:], bf[:])

        def op(name):
            return (class_tiles[name][1][:], class_tiles[name][2][:])

        full = [ps.tile([P, 512], F32, name="full%d" % i) for i in range(4)]
        rowb = [ps.tile([P, 512], F32, name="row%d" % i) for i in range(4)]

        bb_raw = sbuf("bb_raw", [ROWS, PACK, M], F32)
        bb_bf = sbuf("bb_bf", [ROWS, M, PACK], BF16)
        bb_mx = [sbuf("bb_mx%d" % i, [P, M + M // 4], I32) for i in range(4)]
        x_raw = [sbuf("x_raw%d" % g, [P, PACK, N], F32) for g in range(PASSES)]
        a_raw = sbuf("a_raw", [P, PASSES, PACK, R], F32)
        w_raw = {}

        def load_w(g, t0, t1):
            raw = sbuf("w_raw%d%d" % (g, t0), [P, PACK, (t1 - t0) * C], F32)
            nc.sync.dma_start(out=raw[:], in_=w[g * K_PASS:(g + 1) * K_PASS, t0 * C:t1 * C].rearrange("(p j) m -> p j m", j=PACK))
            for t in range(t0, t1):
                w_raw[g, t] = raw[:, :, (t - t0) * C:(t - t0 + 1) * C]

        def load_x(g):
            nc.sync.dma_start(out=x_raw[g][:], in_=x[g * K_PASS:(g + 1) * K_PASS, :].rearrange("(p j) n -> p j n", j=PACK))

        def cx(e, g, t):
            interleave(e, class_tiles["x%d%d" % (g, t)][0][:], x_raw[g][:, :, t * C:(t + 1) * C])

        def cw(e, g, t):
            interleave(e, class_tiles["w%d%d" % (g, t)][0][:], w_raw[g, t])

        def ca(e, g):
            copy(e, class_tiles["a%d" % g][0][:].rearrange("p (b i) j -> p i j b", b=PACK),
                 a_raw[:, g, :, :].rearrange("p j (i b) -> p i j b", b=PACK))

        def zmm(g, t):
            mx(full[t][:, 0:R], op("x%d%d" % (g, t)), op("a%d" % g), g == 0, g == PASSES - 1)

        nc.vector.memset(bb_mx[0][:, M:], 0)
        nc.sync.dma_start(out=bb_raw[:], in_=bb.rearrange("(p j) m -> p j m", j=PACK))
        load_x(0)
        nc.sync.dma_start(out=a_raw[:], in_=a.rearrange("(g p j) r -> p g j r", g=PASSES, j=PACK))
        load_x(1)
        load_w(0, 0, 4)

        interleave("v", bb_bf[:, 0:BB_SPLIT, :], bb_raw[:, :, 0:BB_SPLIT])
        interleave("s", bb_bf[:, BB_SPLIT:, :], bb_raw[:, :, BB_SPLIT:])
        quantize(bb_mx[0][0:ROWS, 0:M], bb_mx[0][0:ROWS, M:].bitcast(U8), bb_bf[:])
        for i in range(1, 4):
            nc.sync.dma_start(out=bb_mx[i][ROWS * i:ROWS * (i + 1), :], in_=bb_mx[0][0:ROWS, :])
        load_w(1, 0, 2)
        load_w(1, 2, 4)

        cx("v", 0, 0)
        cx("s", 0, 2)
        cx("v", 0, 1)
        cx("s", 0, 3)
        for t in range(4):
            q("x0%d" % t)
        ca("v", 0)
        ca("s", 1)
        q("a0")
        q("a1")
        for t in range(4):
            zmm(0, t)

        cx("v", 1, 0)
        cx("s", 1, 1)
        cx("v", 1, 2)
        cx("s", 1, 3)
        for t in range(4):
            q("x1%d" % t)
            zmm(1, t)
        z_t = sbuf("z_t", [P, TILES, R], F32)

        def turn(t):
            nc.vector.transpose(out=z_t[:, t, :], in_=full[t][:, 0:R])

        def cz(t0, t1):
            nc.vector.tensor_copy(out=class_tiles["z"][0][:].rearrange("p (t c i) b -> p t c b i", t=TILES, i=4)[:, t0:t1],
                                  in_=z_t[:].rearrange("p t (b c i) -> p t c b i", b=PACK, i=4)[:, t0:t1])

        turn(0)
        for i in range(11):
            mx(full[0][:, C * (i % 4):C * (i % 4 + 1)], op("x00"), op("a0"), True, True)
        turn(1)
        turn(2)
        turn(3)
        cw("s", 0, 0)
        cw("s", 0, 1)
        cw("s", 0, 2)
        cz(0, 2)
        cz(2, 4)
        q("w00")
        q("z")
        z_codes, z_scales = class_tiles["z"][1], class_tiles["z"][2]

        def rmm():
            for i in range(4):
                for mt in range(4):
                    rows = slice(ROWS * i, ROWS * (i + 1))
                    lhs = (bb_mx[i][rows, mt * C:(mt + 1) * C], bb_mx[i][rows, M:].bitcast(U8)[:, mt * C:(mt + 1) * C])
                    mx(rowb[i][:, mt * C:(mt + 1) * C], lhs, (z_codes[rows, :], z_scales[rows, :]), True, True)

        low = [sbuf("low%d" % h, [P, 4, 2 * C], F32) for h in range(2)]

        def lcopy(e, i, h):
            copy(e, low[h][:, i, :], rowb[i][:, 2 * C * h:2 * C * (h + 1)])

        def wmm(g, mt):
            for t in range(TILES):
                mx(full[mt][:, t * C:(t + 1) * C], op("w%d%d" % (g, mt)), op("x%d%d" % (g, t)),
                   g == 0 and t == 0, g == PASSES - 1 and t == TILES - 1)

        ysum = {}

        def add(mt, t0, t1, bank):
            y = sbuf("y%d%d" % (mt, t0), [P, (t1 - t0) * C], F32)
            ysum[mt, t0] = y
            lo = low[mt // 2][:, :, (mt % 2) * C:(mt % 2 + 1) * C].rearrange("p i (t j) -> p t i j", j=ROWS)[:, t0:t1]
            nc.vector.tensor_tensor(out=y[:].rearrange("p (t i j) -> p t i j", i=4, j=ROWS),
                                    in0=full[bank][:, t0 * C:t1 * C].rearrange("p (t i j) -> p t i j", i=4, j=ROWS),
                                    in1=lo, op=ADD)

        def ad(mt, t0, t1):
            add(mt, t0, t1, mt)

        res = [sbuf("res%d" % mt, [P, N], F32) for mt in range(4)]

        def th(mt, t0, t1):
            nc.scalar.activation(out=res[mt][:, t0 * C:t1 * C], in_=ysum[mt, t0][:], func=TANH)
            if t1 % 2 == 0:
                cols = slice((t1 - 2) * C, t1 * C)
                nc.sync.dma_start(out=out[mt * C:(mt + 1) * C, cols], in_=res[mt][:, cols])

        rmm()
        wmm(0, 0)
        cw("v", 0, 3)
        q("w01")
        wmm(0, 1)
        q("w03")
        q("w02")
        cw("v", 1, 0)
        cw("v", 1, 1)
        for i in range(4):
            lcopy("s", i, 0)
        q("w10")
        wmm(1, 0)
        q("w11")
        wmm(1, 1)
        wmm(0, 2)
        wmm(0, 3)
        lcopy("v", 3, 1)
        lcopy("s", 0, 1)
        lcopy("s", 1, 1)
        cw("v", 1, 2)
        ad(0, 0, 2)
        cw("s", 1, 3)
        lcopy("s", 2, 1)
        ad(0, 2, 4)
        q("w12")
        wmm(1, 2)
        th(0, 0, 2)
        th(0, 2, 4)
        q("w13")
        wmm(1, 3)
        for mt in range(1, 4):
            ad(mt, 0, 2)
            ad(mt, 2, 4)
            th(mt, 0, 2)
            th(mt, 2, 4)
